import numpy as np
import ml_dtypes


def mxq(x, axis, fmt="e4m3"):
    dtype, down = {"e4m3": (ml_dtypes.float8_e4m3fn, 7), "e5m2": (ml_dtypes.float8_e5m2, 14)}[fmt]
    v = np.moveaxis(np.asarray(x, np.float32).astype(ml_dtypes.bfloat16).astype(np.float64), axis, -1)
    blocks = v.reshape(v.shape[:-1] + (-1, 32))
    amax = np.abs(blocks).max(-1, keepdims=True)
    byte = np.maximum(np.where(amax > 0, np.frexp(amax)[1] - 1 + 127, 0) - down, 1)
    scale = np.exp2(byte - 127.0)
    codes = (blocks / scale).astype(np.float32).astype(dtype).astype(np.float64)
    return np.moveaxis((codes * scale).reshape(v.shape), -1, axis)


WIDE = False


def mx_kscale(k):
    if not WIDE:
        return np.ones(k)
    levels = np.array([10, -10, 5, -5, 0])
    if k % 512:
        return np.exp2(np.random.permutation(np.resize(levels, k // 32))).repeat(32)
    a = np.empty((k // 512, 16))
    for p in range(k // 512):
        a[p, :8] = np.random.permutation(np.resize(levels, 8))
        for g in range(8):
            far = levels[np.abs(levels - a[p, g]) >= 10]
            a[p, g + 8] = far[np.random.randint(len(far))]
    return np.exp2(a.ravel()).repeat(32)


def f64(x):
    return np.asarray(x).astype(np.float64)


def striped(idx):
    return np.tile(idx.reshape(-1, 16).T, (8, 1)).astype(np.uint16)


def unstriped(offs):
    return offs[:16].T.reshape(-1).astype(np.int64)


E2M1 = np.array([0.0, 0.5, 1.0, 1.5, 2.0, 3.0, 4.0, 6.0, -0.0, -0.5, -1.0, -1.5, -2.0, -3.0, -4.0, -6.0])


def pack_weight(w, fmt):
    k, n = w.shape
    w = f64(np.asarray(w, np.float32).astype(ml_dtypes.bfloat16)).reshape(k // 32, 32, n)
    amax = np.abs(w).max(1)
    if fmt == "e4m3":
        byte = np.frexp(amax)[1] - 1 + 127 - 7
    else:
        mant, ex = np.frexp(amax / 6.0)
        byte = np.where(mant > 0.5, ex, ex - 1) + 127
    byte = np.clip(np.where(amax > 0, byte, 1), 1, 254)
    scaled = (w * np.exp2(127.0 - byte)[:, None, :]).reshape(k, n).astype(np.float32)
    by_word = np.ascontiguousarray(scaled.reshape(k // 512, 128, 4, n).transpose(0, 1, 3, 2))
    if fmt == "e4m3":
        words = by_word.astype(ml_dtypes.float8_e4m3fn).view(np.uint8)
    else:
        c = by_word.astype(ml_dtypes.float4_e2m1fn).view(np.uint8) & 0xF
        words = (c[..., 0::2] | (c[..., 1::2] << 4)).reshape(k // 512, 128, 2 * n)
    return np.ascontiguousarray(words), np.ascontiguousarray(byte.astype(np.uint8).reshape(k // 512, 16, n))


def unpack_weight(words, scales, fmt):
    g, _, n = scales.shape
    words = np.ascontiguousarray(words).reshape(g, 128, n, -1)
    if fmt == "e4m3":
        vals = words.view(ml_dtypes.float8_e4m3fn).astype(np.float64)
    else:
        nib = np.empty((g, 128, n, 4), np.uint8)
        nib[..., 0::2] = words & 0xF
        nib[..., 1::2] = words >> 4
        vals = E2M1[nib]
    vals = vals * np.repeat(np.exp2(scales.astype(np.float64) - 127.0), 8, axis=1)[..., None]
    return vals.transpose(0, 1, 3, 2).reshape(g * 512, n)


def gelu(v):
    return 0.5 * v * (1.0 + np.tanh(np.sqrt(2.0 / np.pi) * (v + 0.044715 * v**3)))


K, T, S, H, T2, S2, T3, P = 1024, 2048, 512, 1024, 1024, 512, 2048, 512

def setup_inputs():
    n = np.random.standard_normal
    s = mx_kscale(K)[:, None]
    u = mx_kscale(H)[:, None]
    tab_words, tab_scales = pack_weight(n((K, T)) * s, "e4m3")
    w4_words, w4_scales = pack_weight(1.8 * n((H, H)) / np.sqrt(H) / u, "e2m1")
    tab2_words, tab2_scales = pack_weight(n((H, T3)) / np.sqrt(H) / u, "e4m3")
    return {
        "tab_words": tab_words, "tab_scales": tab_scales,
        "offs": striped(np.random.permutation(T)[:S]),
        "w1": (1.5 * n((K, H)) / np.sqrt(K) / s).astype(np.float32),
        "ga": (np.exp(0.3 * n(H)) * u[:, 0]).astype(np.float32),
        "w4_words": w4_words, "w4_scales": w4_scales,
        "gain": (np.exp(0.3 * n(H)) * u[:, 0]).astype(np.float32),
        "wgs": np.exp(0.3 * n((128, S))).astype(np.float32),
        "page0": (1.5 * n((H, T2)) * u).astype(np.float32),
        "tab2_words": tab2_words, "tab2_scales": tab2_scales,
        "offs2": striped(np.random.permutation(T3)[:S2]),
        "offs3": striped(np.random.permutation(T2)[:S]),
        "site": n((S2, P)).astype(np.float32),
        "pos1": striped(np.random.permutation(T2)[:P]),
        "pos2": striped(np.random.permutation(T2)[:P]),
    }

def reference(tab_words, tab_scales, offs, w1, ga, w4_words, w4_scales, gain, wgs, page0,
              tab2_words, tab2_scales, offs2, offs3, site, pos1, pos2):
    v = unpack_weight(tab_words, tab_scales, "e4m3")[:, unstriped(offs)]
    a = mxq(f64(w1), 0, "e4m3").T @ v
    g = f64(ga)[:, None] * np.tanh(a)
    d = unpack_weight(w4_words, w4_scales, "e2m1").T @ mxq(g, 0, "e4m3")
    h = f64(gain)[:, None] * np.maximum(a, d)
    page = f64(page0).copy()
    page[:, unstriped(offs3)] = np.tile(f64(wgs), (H // 128, 1)) * h
    v2 = unpack_weight(tab2_words, tab2_scales, "e4m3")[:, unstriped(offs2)]
    e = v2.T @ mxq(page, 0, "e4m3")
    clone = f64(site) * e[:, unstriped(pos1)]
    return np.maximum(clone, e[:, unstriped(pos2)])

from contextlib import ExitStack

import concourse.mybir as mybir
from concourse.masks import make_identity

K, T, S, H, T2, S2, T3, NP = 1024, 2048, 512, 1024, 1024, 512, 2048, 512
FLOPS = 2 * K * H * S + 2 * H * H * S + 2 * H * S2 * T2

F32 = mybir.dt.float32
BF16 = mybir.dt.bfloat16
I32 = mybir.dt.int32
U32 = mybir.dt.uint32
U16 = mybir.dt.uint16
U8 = mybir.dt.uint8
FP8X4 = mybir.dt.float8_e4m3fn_x4
FP4X4 = mybir.dt.float4_e2m1fn_x4
MULT = mybir.AluOpType.mult
MAX = mybir.AluOpType.max
TANH = mybir.ActivationFunctionType.Tanh
COPY = mybir.ActivationFunctionType.Copy

P = 128
PACK = 4
PASS = P * PACK
NPASS = 2
BANK = 512
JC = 128
NJC = S // JC
SCALAR_COLS = {(0, 0): 0, (1, 0): 0, (0, 1): 48, (1, 1): 40}


def tile_list_clone_site_scores_kernel(
    tc, tab_words, tab_scales, offs, w1, ga, w4_words, w4_scales, gain, wgs, page0,
    tab2_words, tab2_scales, offs2, offs3, site, pos1, pos2, out,
):
    nc = tc.nc
    with ExitStack() as ctx:
        lists = ctx.enter_context(tc.tile_pool(name="lists", bufs=1))
        keep = ctx.enter_context(tc.tile_pool(name="keep", bufs=1))
        psum = ctx.enter_context(tc.psum_pool(name="psum", bufs=1))

        def bank(i, shape, name):
            return psum.tile(shape, F32, name=name, tag="bank%d" % i)

        def load_list(src, name):
            tile = lists.tile([P, S // 16], U16, name=name)
            nc.sync.dma_start(tile[:], src)
            return tile

        def load_words(src, a, name):
            tile = keep.tile([P, T], I32, name=name)
            nc.sync.dma_start(tile[:], src[a].rearrange("p t i -> p (t i)").bitcast(I32))
            return tile

        def load_table_scales(src, name, queue):
            tile = keep.tile([P, src.shape[2]], U8, name=name, tag=name, align_bytes=64)
            nc.vector.memset(tile[:].bitcast(I32), 0)
            for q in range(4):
                queue.dma_start(
                    tile[32 * q : 32 * q + 8, :].bitcast(I32), src[:, 4 * q : 4 * q + 4, :].bitcast(I32)
                )
            return tile

        def load_w1(a, b):
            tile = keep.tile([P, PACK, PASS], F32, name="w1_raw_%d%d" % (a, b), tag="stage", bufs=4)
            rows = w1[a * PASS : (a + 1) * PASS, b * PASS : (b + 1) * PASS]
            nc.sync.dma_start(tile[:], rows.rearrange("(p j) c -> p j c", j=PACK))
            return tile

        def load_channels(src, name):
            tile = keep.tile([P, NPASS, PACK], F32, name=name)
            nc.sync.dma_start(tile[:], src.rearrange("(b p t) -> p b t", b=NPASS, t=PACK))
            return tile

        def gather_words(table, offsets, name):
            tile = keep.tile([P, S], U32, name=name, align_bytes=64)
            nc.vector.tensor_copy(tile[:], table[:].bitcast(U32).indirect(offsets[:]))
            return tile

        def gather_scales(table, offsets, name):
            tile = keep.tile([P, S], U8, name=name, align_bytes=64)
            nc.vector.tensor_copy(tile[:], table[:].indirect(offsets[:]))
            return tile

        ident = keep.tile([P, P], F32)
        make_identity(nc, ident[:])
        tab_s = load_table_scales(tab_scales, "tab_s", nc.gpsimd)
        w4_s_raw = load_table_scales(w4_scales, "w4_s_raw", nc.gpsimd)

        wgs_sb = keep.tile([P, S], F32)
        nc.sync.dma_start(wgs_sb[:], wgs)
        gain_sb = load_channels(gain, "gain_sb")
        w4_raw = keep.tile([P, NPASS, 2 * H], U8)
        nc.sync.dma_start(w4_raw[:].bitcast(I32), w4_words.rearrange("a p c -> p a c").bitcast(I32))
        w1_raw = {}
        tab_w = {}
        w1_raw[0, 0] = load_w1(0, 0)
        tab_w[0] = load_words(tab_words, 0, "tab_w0")
        idx = load_list(offs, "idx")
        w1_raw[1, 0] = load_w1(1, 0)
        tab_w[1] = load_words(tab_words, 1, "tab_w1")
        ga_sb = load_channels(ga, "ga_sb")
        w1_raw[0, 1] = load_w1(0, 1)
        w1_raw[1, 1] = load_w1(1, 1)
        idx3 = load_list(offs3, "idx3")
        page = {}
        for b in range(NPASS):
            rows = page0[b * PASS : (b + 1) * PASS, :].rearrange("(p t) c -> t p c", t=PACK)
            for t in range(PACK):
                page[b, t] = keep.tile([P, T2], F32, name="page_%d%d" % (b, t))
                nc.sync.dma_start(page[b, t][:], rows[t])
        idx2 = load_list(offs2, "idx2")
        tab2_s = load_table_scales(tab2_scales, "tab2_s", nc.sync)
        tab2_w = [load_words(tab2_words, a, "tab2_w%d" % a) for a in range(NPASS)]
        p1 = load_list(pos1, "p1")
        p2 = load_list(pos2, "p2")

        turned = bank(0, [P, NJC, P], "turned")
        for jc in range(NJC):
            nc.tensor.transpose(turned[:, jc, :], wgs_sb[:, jc * JC : (jc + 1) * JC], ident[:])
        spread = keep.tile([P, NJC, PACK, 4, 32], F32, tag="spread_site")
        for rep in range(4):
            nc.scalar.copy(spread[:, :, :, rep, :], turned[:].rearrange("p c (q t) -> p c t q", t=PACK))
        wg = {}
        for t in range(PACK):
            dealt = bank(4 + t, [P, NJC, JC], "dealt%d" % t)
            for jc in range(NJC):
                nc.tensor.transpose(dealt[:, jc, :], spread[:, jc, t, :, :].rearrange("p r q -> p (r q)"), ident[:])
            for b in range(NPASS):
                wg[b, t] = keep.tile([P, S], F32, name="wg_%d%d" % (b, t))
                nc.scalar.activation(
                    wg[b, t][:], dealt[:].rearrange("p c j -> p (c j)"), COPY, scale=gain_sb[:, b, t : t + 1]
                )
        site_sb = keep.tile([P, S2 // P, NP], F32, tag="spread_site")
        nc.sync.dma_start(site_sb[:], site.rearrange("(m p) j -> p m j", p=P))

        w4_w = keep.tile([P, NPASS * 2 * H], U8, align_bytes=64)
        nc.vector.tensor_copy(
            w4_w[:].bitcast(U16).rearrange("p (g t q) -> p g t q", t=PACK, q=P),
            w4_raw[:].rearrange("p a c -> p (a c)").bitcast(U16).rearrange("p (g q t) -> p g t q", t=PACK, q=P),
        )

        w1_c = {}
        w1_s = {}

        def quantise_w1(a, b):
            woven = keep.tile([P, PACK, P, PACK], BF16, name="w1_bf_%d%d" % (a, b), tag="woven", bufs=2, align_bytes=64)
            src = w1_raw[a, b][:].rearrange("p j (m t) -> p m t j", t=PACK)
            dst = woven[:].rearrange("p t m j -> p m t j")
            cut = SCALAR_COLS[a, b]
            if cut:
                nc.scalar.copy(dst[:, :cut], src[:, :cut])
            nc.vector.tensor_copy(dst[:, cut:], src[:, cut:])
            w1_c[a, b] = keep.tile([P, PASS], U32, name="w1_c_%d%d" % (a, b), align_bytes=64)
            w1_s[a, b] = keep.tile([P, PASS], U8, name="w1_s_%d%d" % (a, b), align_bytes=64)
            nc.vector.quantize_mx(
                w1_c[a, b][:].bitcast(FP8X4), w1_s[a, b][:], woven[:].rearrange("p t m j -> p (t m j)")
            )

        acc_a = {}

        def first_product(a, b):
            for jc in range(NJC):
                if a == 0:
                    acc_a[b, jc] = bank(4 * b + jc, [P, PACK, JC], "a_%d%d" % (b, jc))
                cols = slice(jc * JC, (jc + 1) * JC)
                for t in range(PACK):
                    wc = slice(t * P, (t + 1) * P)
                    nc.tensor.matmul_mx(
                        acc_a[b, jc][:, t, :],
                        lhsT=w1_c[a, b][:, wc].bitcast(FP8X4), lhsT_scale=w1_s[a, b][:, wc],
                        rhs=v_w[a][:, cols].bitcast(FP8X4), rhs_scale=v_s[4 * a :, cols],
                        start=(a == 0 and t == 0), stop=(a == NPASS - 1 and t == PACK - 1),
                    )

        g_c = [keep.tile([P, S], U32, name="g_c%d" % b, align_bytes=64) for b in range(NPASS)]
        g_s = [keep.tile([P, S], U8, name="g_s%d" % b, align_bytes=64) for b in range(NPASS)]
        a_sb = [keep.tile([P, PACK, S], F32, name="a_sb%d" % b) for b in range(NPASS)]

        def make_g(b):
            gb = {}
            for jc in range(NJC + 1):
                if jc < NJC:
                    th = keep.tile([P, JC, PACK], F32, name="th_%d%d" % (b, jc), tag="th", bufs=3)
                    nc.scalar.activation(th[:], acc_a[b, jc][:].rearrange("p t j -> p j t"), TANH)
                    gb[jc] = keep.tile([P, JC, PACK], BF16, name="gb_%d%d" % (b, jc), tag="gb", bufs=4, align_bytes=64)
                    nc.vector.tensor_tensor(
                        gb[jc][:], th[:], ga_sb[:, b : b + 1, :].to_broadcast([P, JC, PACK]), MULT
                    )
                if jc > 0:
                    cols = slice((jc - 1) * JC, jc * JC)
                    nc.vector.quantize_mx(
                        g_c[b][:, cols].bitcast(FP8X4), g_s[b][:, cols], gb[jc - 1][:].rearrange("p j t -> p (j t)")
                    )

        def keep_a(b):
            for jc in range(NJC):
                nc.scalar.copy(a_sb[b][:, :, jc * JC : (jc + 1) * JC], acc_a[b, jc][:])

        v_w = {}
        quantise_w1(0, 0)
        v_w[0] = gather_words(tab_w[0], idx, "v_w0")
        v_s = gather_scales(tab_s, idx, "v_s")
        first_product(0, 0)
        quantise_w1(1, 0)
        v_w[1] = gather_words(tab_w[1], idx, "v_w1")
        first_product(1, 0)
        w4_s = [
            keep.tile([P, H], U8, name="w4_s0", tag="tab_s", align_bytes=64),
            keep.tile([P, H], U8, name="w4_s1", align_bytes=64),
        ]
        nc.vector.tensor_copy(
            w4_s[0][:].rearrange("p (b t q) -> p b t q", t=PACK, q=P),
            w4_s_raw[:].rearrange("p (b q t) -> p b t q", t=PACK, q=P),
        )
        for q in range(4):
            nc.gpsimd.dma_start(
                w4_s[1][32 * q : 32 * q + 4, :].bitcast(I32), w4_s[0][32 * q + 4 : 32 * q + 8, :].bitcast(I32)
            )
        quantise_w1(0, 1)
        first_product(0, 1)
        quantise_w1(1, 1)
        first_product(1, 1)
        make_g(0)
        make_g(1)
        keep_a(0)

        acc_d = {}

        def second_product(a, b):
            for t in range(PACK):
                if a == 0:
                    acc_d[b, t] = bank(4 * b + t, [P, S], "d_%d%d" % (b, t))
                c0 = a * H + b * PASS + t * P
                nc.tensor.matmul_mx(
                    acc_d[b, t][:],
                    lhsT=w4_w[:, 2 * c0 : 2 * (c0 + P)].bitcast(FP4X4), lhsT_scale=w4_s[a][:, c0 - a * H : c0 - a * H + P],
                    rhs=g_c[a][:].bitcast(FP8X4), rhs_scale=g_s[a][:],
                    start=(a == 0), stop=(a == NPASS - 1),
                )

        second_product(0, 0)
        second_product(1, 0)
        keep_a(1)
        second_product(0, 1)
        second_product(1, 1)

        page_bf = {}
        page_c = [keep.tile([P, T2], U32, name="page_c%d" % b, align_bytes=64) for b in range(NPASS)]
        page_s = [keep.tile([P, T2], U8, name="page_s%d" % b, align_bytes=64) for b in range(NPASS)]
        tiles = [(b, t) for b in range(NPASS) for t in range(PACK)]
        larger = {}

        def take_max(b, t):
            larger[b, t] = keep.tile([P, S], F32, name="larger_%d%d" % (b, t), tag="work", bufs=3)
            nc.vector.tensor_tensor(larger[b, t][:], acc_d[b, t][:], a_sb[b][:, t, :], MAX)

        def place(b, t):
            nc.vector.tensor_tensor(page[b, t][:].indirect(idx3[:]), larger[b, t][:], wg[b, t][:], MULT)
            if t == 0:
                page_bf[b] = keep.tile([P, T2, PACK], BF16, name="page_bf%d" % b, tag="woven", bufs=2, align_bytes=64)
            for h in range(2):
                cols = slice(h * BANK, (h + 1) * BANK)
                nc.scalar.copy(page_bf[b][:, cols, t], page[b, t][:, cols])

        def quantise_page(b, h):
            cols = slice(h * BANK, (h + 1) * BANK)
            nc.vector.quantize_mx(
                page_c[b][:, cols].bitcast(FP8X4), page_s[b][:, cols],
                page_bf[b][:, cols, :].rearrange("p c t -> p (c t)"),
            )

        v2_w = {}
        take_max(*tiles[0])
        for i in range(len(tiles)):
            if i + 1 < len(tiles):
                take_max(*tiles[i + 1])
            place(*tiles[i])
            if tiles[i] == (1, 1):
                v2_s = gather_scales(tab2_s, idx2, "v2_s")
                v2_w[0] = gather_words(tab2_w[0], idx2, "v2_w0")

        v2_w[1] = gather_words(tab2_w[1], idx2, "v2_w1")
        for h in range(2):
            quantise_page(0, h)
            quantise_page(1, h)
        acc_e = {}
        e_sb = {}
        for m in range(S2 // P):
            rows = slice(m * P, (m + 1) * P)
            e_sb[m] = keep.tile([P, T2], F32, name="e_%d" % m, tag="stage", bufs=4)
            for h in range(2):
                cols = slice(h * BANK, (h + 1) * BANK)
                for a in range(NPASS):
                    if a == 0:
                        acc_e[m, h] = bank(2 * m + h, [P, BANK], "e_acc_%d%d" % (m, h))
                    nc.tensor.matmul_mx(
                        acc_e[m, h][:],
                        lhsT=v2_w[a][:, rows].bitcast(FP8X4), lhsT_scale=v2_s[4 * a :, rows],
                        rhs=page_c[a][:, cols].bitcast(FP8X4), rhs_scale=page_s[a][:, cols],
                        start=(a == 0), stop=(a == NPASS - 1),
                    )
                    if a == 1:
                        nc.scalar.copy(e_sb[m][:, cols], acc_e[m, h][:])

        clone = {}
        check = {}

        def pick_clone(m):
            clone[m] = keep.tile([P, NP], F32, name="clone_%d" % m, tag="work", bufs=3)
            nc.vector.tensor_tensor(clone[m][:], e_sb[m][:].indirect(p1[:]), site_sb[:, m, :], MULT)

        pick_clone(0)
        for m in range(S2 // P):
            check[m] = keep.tile([P, NP], F32, name="check_%d" % m, tag="check", bufs=2)
            nc.vector.tensor_copy(check[m][:], e_sb[m][:].indirect(p2[:]))
            if m + 1 < S2 // P:
                pick_clone(m + 1)
            best = keep.tile([P, NP], F32, name="best_%d" % m, tag="best", bufs=2)
            nc.vector.tensor_tensor(best[:], clone[m][:], check[m][:], MAX)
            nc.sync.dma_start(out[m * P : (m + 1) * P, :], best[:])
